import numpy as np, ml_dtypes
CORES = [88,96,104,112,120,216,224,232,240,248]
N = 10
import mx_ref
NC, G = 256, 2
C = np.float32(0.0329)
FROM = [[4,7,0,1,8,2,9,6,5,3],[8,9,5,4,7,0,3,6,1,2],[1,8,4,0,9,2,7,5,3,6]]
BF = ml_dtypes.bfloat16
def cut(t, i, w=512):
    return t[:, w * i:w * i + w]
def tile(rs):
    return np.stack(rs, axis=2).reshape(128, -1).astype(BF)
def layer(w, X):
    out = []
    for i in range(G):
        for t in range(len(X)):
            p = mx_ref.matmul(mx_ref.quantize(cut(w, len(X) * i + t)), X[t])
            z = p if t == 0 else z + p
        out.append(z)
    return out
def act(Z):
    return [np.maximum(s * z, 0) * C for z in Z for s in (1, -1)]
def setup_inputs(rng):
    def f(*shape):
        return mx_ref.flush((rng.standard_normal(shape, dtype=np.float32) * np.exp2(rng.integers(-2, 3, shape[:-1] + (1,)))).astype(BF))
    return {"x": f(N, 128, 4 * NC), "w": f(N, 128, 2 * 2 * G * 512), "v": f(N, 128, 2 * 512)}
def setup_inputs_blocks(rng):
    d = setup_inputs(rng)
    for k in ("x", "v"): d[k] = mx_ref.spread(d[k], rng, 4)
    for k in ("w",): d[k] = mx_ref.spread(d[k], rng, 2)
    return d
def setup_inputs_wide(rng):
    d = setup_inputs(rng)
    for k in ("x", "w", "v"): d[k] = mx_ref.flush((d[k].astype(np.float32) * np.exp2(rng.integers(-5, 6, (N, 1, 1))).astype(np.float32)).astype(BF))
    return d
def reference(x, w, v):
    a = [mx_ref.quantize(x[r]) for r in range(N)]
    for l in range(2):
        a = [mx_ref.quantize(tile(act(layer(cut(w[r], l, 2 * G * 512), [a[r], a[FROM[l][r]]])))) for r in range(N)]
    y = np.zeros((N, 128, NC), np.float32)
    for r in range(N):
        y[r] = mx_ref.matmul(mx_ref.quantize(cut(v[r], 0)), a[r]) + mx_ref.matmul(mx_ref.quantize(cut(v[r], 1)), a[FROM[2][r]])
    return {"y": y}

@@ -1,0 +1,242 @@
+from concourse.bass import DstId, RemoteDMATransfer
+from concourse.mybir import dt, AluOpType, ActivationFunctionType
+
+WORLD = 256
+NC = 256
+H = 2
+C = 0.0329
+SHADOW = (1, 2)
+NE_ON, NE_OFF = 8, 8
+EARLY_W1 = True
+SECOND_COPY = True
+GATE = True
+VIA = False
+
+SCRATCH = {
+    "xt": ("sbuf", [128, 4 * NC], "bfloat16"),
+    "wt": ("sbuf", [128, 4096], "bfloat16"),
+    "vt": ("sbuf", [128, 1024], "bfloat16"),
+    "wq": ("sbuf", [128, 1024], "float8_e4m3fn_x4"),
+    "wp": ("sbuf", [128, 1024], "uint8"),
+    "vq": ("sbuf", [128, 256], "float8_e4m3fn_x4"),
+    "vp": ("sbuf", [128, 256], "uint8"),
+    "h1": ("sbuf", [128, 4 * NC], "bfloat16"),
+    "h2": ("sbuf", [128, 4 * NC], "bfloat16"),
+    "yt": ("sbuf", [128, NC], "float32"),
+    "z": ("psum", [128, 4096], "float32"),
+}
+for _l in range(3):
+    for _k in ("o", "p"):
+        SCRATCH["%sq%d" % (_k, _l)] = ("sbuf", [128, NC], "float8_e4m3fn_x4")
+        SCRATCH["%sp%d" % (_k, _l)] = ("sbuf", [128, NC], "uint8")
+
+SEMAPHORES = ["sent", "gate", "lv", "qv"]
+SEMAPHORES += ["%s%d" % (k, p) for k in ("lw", "qw", "sw") for p in range(4)]
+SEMAPHORES += ["%s%d" % (k, h) for k in ("lx", "zy", "cy", "st") for h in range(2)]
+SEMAPHORES += ["%s%d%d" % (k, l, h) for k in ("o", "p") for l in range(3) for h in range(2)]
+SEMAPHORES += ["a%d%d" % (l, h) for l in range(2) for h in range(2)]
+SEMAPHORES += ["z%d%d%d" % (l, i, h) for l in range(2) for i in range(2) for h in range(2)]
+
+
+def _engines(topo, src, dst, far, alone):
+    m = topo.mask(src, dst)
+    away = topo.mask(src, far)
+    on_chip = m != away
+    stay = [b for b in range(m.bit_length()) if (m & ~away) >> b & 1]
+    bits = stay + [b for b in range(m.bit_length()) if (m & away) >> b & 1]
+    n = min(NE_ON if on_chip else NE_OFF, len(bits) if alone or not on_chip else len(stay))
+    return sum(1 << b for b in bits[:n]), n
+
+
+def _plan(T, topo):
+    cores, FROM = list(T.cores), T.tables["FROM"]
+    n, L, cw = len(cores), len(FROM), NC // H
+    to = [[FROM[l].index(r) for r in range(n)] for l in range(L)]
+    helper = [next(k for k in range(WORLD) if k not in cores and topo.host(k) == topo.host(c) and topo.chip(k) == topo.chip(c)
+                   and topo.die(k) == topo.die(c) and all(topo.may_write(k, d) for d in cores)) for c in cores]
+    maker = [[helper[r] if l in SHADOW and not topo.may_write(cores[r], cores[to[l][r]]) else cores[r]
+              for r in range(n)] for l in range(L)]
+    rank, far = {}, {}
+    for r in range(n):
+        rank[cores[r]] = rank[helper[r]] = r
+        for k in (cores[r], helper[r]):
+            far[k] = next(d for d in cores if d != cores[r] and topo.may_write(k, d))
+    steps, need, alias = {k: [] for k in rank}, {k: {} for k in rank}, {k: {} for k in rank}
+
+    def add(src, key, waits, outs, early=False):
+        steps[src].append((key, waits, outs, early))
+        for o in outs:
+            need[o[0]][o[5]] = need[o[0]].get(o[5], 0) + 2 * _engines(topo, src, o[0], far[src], len(outs) == 1)[1]
+
+    for l in range(L):
+        for r in range(n):
+            c, hp, d, m = cores[r], helper[r], to[l][r], maker[l][r]
+            tgt = maker[l + 1][d] if l + 1 < L else cores[d]
+            keep = l + 1 < L and maker[l + 1][r] == hp and m == c
+            direct = topo.may_write(m, tgt) and not (VIA and l == 0 and hp in [maker[k][r] for k in range(L)])
+            own, par = "o%d" % l, "p%d" % l
+            for h in range(H):
+                a, b = h * cw, h * cw + cw
+                outs = [(tgt, own, par, a, b, "%s%d" % (par, h))] if direct else []
+                if keep or not direct:
+                    outs.append((hp, own, own, a, b, "%s%d" % (own, h)))
+                add(m, (l - 1, 1, h, 1), ["%s%d" % (own, h)], outs, l == 0)
+                if not direct:
+                    add(hp, (l, 0, h, 0), ["%s%d" % (own, h)], [(tgt, own, par, a, b, "%s%d" % (par, h))])
+                if tgt != cores[d] and not SECOND_COPY:
+                    add(tgt, (l, 1, h, 0), ["%s%d" % (par, h)], [(cores[d], par, par, a, b, "%s%d" % (par, h))])
+            if tgt != cores[d] and SECOND_COPY:
+                add(m if direct else hp, (l - 1, 1, H, 2) if direct else (l, 0, H, 1), ["%s%d" % (own, h) for h in range(H)],
+                    [(cores[d], own, par, 0, NC, par + "0")])
+                for h in range(1, H):
+                    alias[cores[d]]["%s%d" % (par, h)] = par + "0"
+    early = []
+    for r in range(n):
+        c, hp = cores[r], helper[r]
+        waits_long = maker[1][r] == hp or (maker[2][r] == hp and not topo.may_write(cores[FROM[0][r]], c))
+        early.append(EARLY_W1 and waits_long)
+        for l in range(L - 1):
+            if maker[l + 1][r] == hp:
+                for p in (2 * l, 2 * l + 1):
+                    key = (-1, 2, p, 0) if l == 0 or early[r] else (l - 1, 2, p, 0)
+                    add(c, key, ["qw%d" % p], [(hp, "w", "w", 256 * p, 256 * p + 256, "sw%d" % p)], l == 0)
+    return {"rank": rank, "far": far, "steps": steps, "need": need, "alias": alias, "maker": maker, "early": early}
+
+
+def rank_program(g, core, T, topo):
+    if not any(topo.host(c) == topo.host(core) and topo.chip(c) == topo.chip(core) for c in T.cores):
+        return
+    plan = _plan(T, topo)
+    if core not in plan["rank"]:
+        return
+    r, need, alias, maker, cw = plan["rank"][core], plan["need"][core], plan["alias"][core], plan["maker"], NC // H
+    main = core == T.cores[r]
+    seen = {}
+
+    def wait(q, sem, val=None):
+        sem = alias.get(sem, sem)
+        val = need.get(sem, 1) if val is None else val
+        if seen.get((q, sem), 0) < val:
+            seen[(q, sem)] = val
+            {"g": g, "t": g.tensor, "v": g.vector, "s": g.scalar, "y": g.sync}[q].wait_ge(T.sem[sem], val)
+
+    def bank(b):
+        return T.z[:, 512 * b:512 * b + cw]
+
+    def products(l):
+        for t, k in enumerate(("o", "p")):
+            for h in range(H):
+                wait("t", "%s%d%d" % (k, l, h))
+                for i in range(2):
+                    j = 4 * l + 2 * i + t
+                    wait("t", "%s%d" % ("qw" if main else "sw", j // 2))
+                    ins = g.tensor.matmul_mx(bank((2 * l + i) * H + h), T.wq[:, 128 * j:128 * j + 128], T.wp[:, 128 * j:128 * j + 128],
+                                             T["%sq%d" % (k, l)][:, h * cw:h * cw + cw], T["%sp%d" % (k, l)][:, h * cw:h * cw + cw],
+                                             t == 0, t == 1)
+                    if t == 1:
+                        ins.then_inc(T.sem["z%d%d%d" % (l, i, h)], 1)
+
+    def tile(l):
+        ht = T["h%d" % (l + 1)]
+        for h in range(H):
+            a, b, done = 4 * h * cw, 4 * (h + 1) * cw, T.sem["a%d%d" % (l, h)]
+            z0, z1 = bank(2 * l * H + h), bank((2 * l + 1) * H + h)
+            wait("v", "z%d0%d" % (l, h))
+            g.vector.tensor_scalar(ht[:, a:b:4], z0, 0.0, C, AluOpType.max, AluOpType.mult).then_inc(done, 1)
+            g.vector.tensor_scalar(ht[:, a + 1:b:4], z0, -C, 0.0, AluOpType.mult, AluOpType.max).then_inc(done, 1)
+            wait("s", "z%d1%d" % (l, h))
+            g.scalar.activation(ht[:, a + 2:b:4], z1, ActivationFunctionType.Relu, scale=C).then_inc(done, 1)
+            g.scalar.activation(ht[:, a + 3:b:4], z1, ActivationFunctionType.Relu, scale=-C).then_inc(done, 1)
+            wait("v", "a%d%d" % (l, h), 4)
+            g.vector.quantize_mx(T["oq%d" % (l + 1)][:, h * cw:h * cw + cw], T["op%d" % (l + 1)][:, h * cw:h * cw + cw],
+                                 ht[:, a:b]).then_inc(T.sem["o%d%d" % (l + 1, h)], 1)
+
+    def pack_w(p):
+        wait("v", "lw%d" % p, 16)
+        g.vector.quantize_mx(T.wq[:, 256 * p:256 * p + 256], T.wp[:, 256 * p:256 * p + 256],
+                             T.wt[:, 1024 * p:1024 * p + 1024]).then_inc(T.sem["qw%d" % p], 1)
+
+    names = lambda k: ("wq", "wp") if k == "w" else (k[0] + "q" + k[1], k[0] + "p" + k[1])
+    calls, left = [], {"sent": 0, "gate": 0}
+    for key, waits, outs, first in sorted(plan["steps"][core], key=lambda s: s[0]):
+        mine = "gate" if first and GATE and main else "sent"
+        for part in range(2):
+            trs = []
+            for dst, src_k, dst_k, a, b, there in outs:
+                mask, ne = _engines(topo, core, dst, plan["far"][core], len(outs) == 1)
+                rid, pid = topo.addr(dst, core)
+                s_ap, d_ap = T[names(src_k)[part]][:, a:b], T[names(dst_k)[part]][:, a:b]
+                if part == 0:
+                    s_ap, d_ap = s_ap.bitcast(dt.uint8), d_ap.bitcast(dt.uint8)
+                trs.append((d_ap, s_ap, T.sem[there], pid, rid, mask))
+                left[mine] += ne
+            calls.append((waits, trs, mine))
+
+    if main:
+        early = plan["early"][r]
+        for h in range(H):
+            g.sync.dma_start(T.xt[:, 4 * h * cw:4 * (h + 1) * cw], T.x[:, 4 * h * cw:4 * (h + 1) * cw]).then_inc(T.sem["lx%d" % h], 16)
+        for p in range(4):
+            if p == 2 and left["gate"]:
+                wait("y", "gate", left["gate"])
+            g.sync.dma_start(T.wt[:, 1024 * p:1024 * p + 1024], T.w[:, 1024 * p:1024 * p + 1024]).then_inc(T.sem["lw%d" % p], 16)
+        g.sync.dma_start(T.vt[:], T.v[:]).then_inc(T.sem.lv, 16)
+        for h in range(H):
+            wait("v", "lx%d" % h, 16)
+            g.vector.quantize_mx(T.oq0[:, h * cw:h * cw + cw], T.op0[:, h * cw:h * cw + cw],
+                                 T.xt[:, 4 * h * cw:4 * (h + 1) * cw]).then_inc(T.sem["o0%d" % h], 1)
+        pack_w(0)
+        pack_w(1)
+        if early:
+            pack_w(2)
+            pack_w(3)
+        products(0)
+        tile(0)
+        if not early:
+            pack_w(2)
+            pack_w(3)
+        products(1)
+        tile(1)
+        wait("v", "lv", 16)
+        g.vector.quantize_mx(T.vq[:], T.vp[:], T.vt[:]).then_inc(T.sem.qv, 1)
+        base = 4 * H if 5 * H <= 8 else 0
+        for t, k in enumerate(("o", "p")):
+            for h in range(H):
+                wait("t", "%s2%d" % (k, h))
+                wait("t", "qv", 1)
+                ins = g.tensor.matmul_mx(bank(base + h), T.vq[:, 128 * t:128 * t + 128], T.vp[:, 128 * t:128 * t + 128],
+                                         T["%sq2" % k][:, h * cw:h * cw + cw], T["%sp2" % k][:, h * cw:h * cw + cw], t == 0, t == 1)
+                if t == 1:
+                    ins.then_inc(T.sem["zy%d" % h], 1)
+        for h in range(H):
+            yv = T.yt[:, h * cw:h * cw + cw]
+            if h % 2 == 0:
+                wait("v", "zy%d" % h, 1)
+                g.vector.tensor_copy(yv, bank(base + h)).then_inc(T.sem["cy%d" % h], 1)
+                wait("y", "cy%d" % h, 1)
+                g.sync.dma_start(T.y[:, h * cw:h * cw + cw], yv).then_inc(T.sem["st%d" % h], 16)
+            else:
+                wait("s", "zy%d" % h, 1)
+                g.scalar.activation(yv, bank(base + h), ActivationFunctionType.Copy).then_inc(T.sem["cy%d" % h], 1)
+                wait("s", "cy%d" % h, 1)
+                g.scalar.dma_start(T.y[:, h * cw:h * cw + cw], yv).then_inc(T.sem["st%d" % h], 16)
+        for h in range(H):
+            wait("y" if h % 2 == 0 else "s", "st%d" % h, 16)
+    else:
+        for l in range(2):
+            if maker[l + 1][r] == core:
+                products(l)
+                tile(l)
+
+    for waits, trs, mine in calls:
+        for sem in waits:
+            wait("g", sem)
+        if len(trs) == 1:
+            d_ap, s_ap, there, pid, rid, mask = trs[0]
+            g.remote_dma(d_ap, s_ap, there, T.sem[mine], pid, rid, mask)
+        else:
+            g.remote_dma_fused([RemoteDMATransfer(dst_ids=[DstId(rid=rid, pnc=pid)], dma_engine_mask=mask, remote_sem=there,
+                                                  src=s_ap, dst=d_ap) for d_ap, s_ap, there, pid, rid, mask in trs],
+                               local_sem=T.sem[mine])
+    if left["sent"]:
+        g.wait_ge(T.sem.sent, left["sent"])

@@ -5,12 +5,6 @@ WORLD = 256
 NC = 256
 H = 2
 C = 0.0329
-SHADOW = (1, 2)
-NE_ON, NE_OFF = 8, 8
-EARLY_W1 = True
-SECOND_COPY = True
-GATE = True
-VIA = False
 
 SCRATCH = {
     "xt": ("sbuf", [128, 4 * NC], "bfloat16"),
@@ -30,7 +24,7 @@ for _l in range(3):
         SCRATCH["%sq%d" % (_k, _l)] = ("sbuf", [128, NC], "float8_e4m3fn_x4")
         SCRATCH["%sp%d" % (_k, _l)] = ("sbuf", [128, NC], "uint8")
 
-SEMAPHORES = ["sent", "gate", "lv", "qv"]
+SEMAPHORES = ["sent", "gate", "lv", "qv", "oc", "os"]
 SEMAPHORES += ["%s%d" % (k, p) for k in ("lw", "qw", "sw") for p in range(4)]
 SEMAPHORES += ["%s%d" % (k, h) for k in ("lx", "zy", "cy", "st") for h in range(2)]
 SEMAPHORES += ["%s%d%d" % (k, l, h) for k in ("o", "p") for l in range(3) for h in range(2)]
@@ -38,83 +32,34 @@ SEMAPHORES += ["a%d%d" % (l, h) for l in range(2) for h in range(2)]
 SEMAPHORES += ["z%d%d%d" % (l, i, h) for l in range(2) for i in range(2) for h in range(2)]
 
 
-def _engines(topo, src, dst, far, alone):
-    m = topo.mask(src, dst)
-    away = topo.mask(src, far)
-    on_chip = m != away
-    stay = [b for b in range(m.bit_length()) if (m & ~away) >> b & 1]
-    bits = stay + [b for b in range(m.bit_length()) if (m & away) >> b & 1]
-    n = min(NE_ON if on_chip else NE_OFF, len(bits) if alone or not on_chip else len(stay))
-    return sum(1 << b for b in bits[:n]), n
+def _lanes(cores, topo, c):
+    can = [k for k in range(WORLD) if k not in cores and topo.host(k) == topo.host(c) and topo.chip(k) == topo.chip(c)
+           and all(topo.may_write(k, d) for d in cores)]
+    near = [k for k in can if topo.die(k) == topo.die(c)]
+    away = [k for k in can if topo.die(k) != topo.die(c)]
+    return (near + away)[0], (away + near[1:])[0]
 
 
-def _plan(T, topo):
-    cores, FROM = list(T.cores), T.tables["FROM"]
-    n, L, cw = len(cores), len(FROM), NC // H
-    to = [[FROM[l].index(r) for r in range(n)] for l in range(L)]
-    helper = [next(k for k in range(WORLD) if k not in cores and topo.host(k) == topo.host(c) and topo.chip(k) == topo.chip(c)
-                   and topo.die(k) == topo.die(c) and all(topo.may_write(k, d) for d in cores)) for c in cores]
-    maker = [[helper[r] if l in SHADOW and not topo.may_write(cores[r], cores[to[l][r]]) else cores[r]
-              for r in range(n)] for l in range(L)]
-    rank, far = {}, {}
-    for r in range(n):
-        rank[cores[r]] = rank[helper[r]] = r
-        for k in (cores[r], helper[r]):
-            far[k] = next(d for d in cores if d != cores[r] and topo.may_write(k, d))
-    steps, need, alias = {k: [] for k in rank}, {k: {} for k in rank}, {k: {} for k in rank}
-
-    def add(src, key, waits, outs, early=False):
-        steps[src].append((key, waits, outs, early))
-        for o in outs:
-            need[o[0]][o[5]] = need[o[0]].get(o[5], 0) + 2 * _engines(topo, src, o[0], far[src], len(outs) == 1)[1]
-
-    for l in range(L):
-        for r in range(n):
-            c, hp, d, m = cores[r], helper[r], to[l][r], maker[l][r]
-            tgt = maker[l + 1][d] if l + 1 < L else cores[d]
-            keep = l + 1 < L and maker[l + 1][r] == hp and m == c
-            direct = topo.may_write(m, tgt) and not (VIA and l == 0 and hp in [maker[k][r] for k in range(L)])
-            own, par = "o%d" % l, "p%d" % l
-            for h in range(H):
-                a, b = h * cw, h * cw + cw
-                outs = [(tgt, own, par, a, b, "%s%d" % (par, h))] if direct else []
-                if keep or not direct:
-                    outs.append((hp, own, own, a, b, "%s%d" % (own, h)))
-                add(m, (l - 1, 1, h, 1), ["%s%d" % (own, h)], outs, l == 0)
-                if not direct:
-                    add(hp, (l, 0, h, 0), ["%s%d" % (own, h)], [(tgt, own, par, a, b, "%s%d" % (par, h))])
-                if tgt != cores[d] and not SECOND_COPY:
-                    add(tgt, (l, 1, h, 0), ["%s%d" % (par, h)], [(cores[d], par, par, a, b, "%s%d" % (par, h))])
-            if tgt != cores[d] and SECOND_COPY:
-                add(m if direct else hp, (l - 1, 1, H, 2) if direct else (l, 0, H, 1), ["%s%d" % (own, h) for h in range(H)],
-                    [(cores[d], own, par, 0, NC, par + "0")])
-                for h in range(1, H):
-                    alias[cores[d]]["%s%d" % (par, h)] = par + "0"
-    early = []
-    for r in range(n):
-        c, hp = cores[r], helper[r]
-        waits_long = maker[1][r] == hp or (maker[2][r] == hp and not topo.may_write(cores[FROM[0][r]], c))
-        early.append(EARLY_W1 and waits_long)
-        for l in range(L - 1):
-            if maker[l + 1][r] == hp:
-                for p in (2 * l, 2 * l + 1):
-                    key = (-1, 2, p, 0) if l == 0 or early[r] else (l - 1, 2, p, 0)
-                    add(c, key, ["qw%d" % p], [(hp, "w", "w", 256 * p, 256 * p + 256, "sw%d" % p)], l == 0)
-    return {"rank": rank, "far": far, "steps": steps, "need": need, "alias": alias, "maker": maker, "early": early}
+def _bits(m):
+    return [b for b in range(m.bit_length()) if m >> b & 1]
 
 
 def rank_program(g, core, T, topo):
-    if not any(topo.host(c) == topo.host(core) and topo.chip(c) == topo.chip(core) for c in T.cores):
+    cores, FROM = list(T.cores), T.tables["FROM"]
+    here = [r for r, c in enumerate(cores) if topo.host(c) == topo.host(core) and topo.chip(c) == topo.chip(core)]
+    if not here:
         return
-    plan = _plan(T, topo)
-    if core not in plan["rank"]:
+    r = here[0]
+    lanes = [_lanes(cores, topo, c) for c in cores]
+    main = core == cores[r]
+    if not main and core not in lanes[r]:
         return
-    r, need, alias, maker, cw = plan["rank"][core], plan["need"][core], plan["alias"][core], plan["maker"], NC // H
-    main = core == T.cores[r]
-    seen = {}
+    cw = NC // H
+    lane = None if main else lanes[r].index(core)
+    to = [FROM[l].index(r) for l in range(3)]
+    need, seen, left = {}, {}, {"sent": 0, "gate": 0}
 
     def wait(q, sem, val=None):
-        sem = alias.get(sem, sem)
         val = need.get(sem, 1) if val is None else val
         if seen.get((q, sem), 0) < val:
             seen[(q, sem)] = val
@@ -123,10 +68,14 @@ def rank_program(g, core, T, topo):
     def bank(b):
         return T.z[:, 512 * b:512 * b + cw]
 
-    def products(l):
+    def own(l, h):
+        return ("oc", "os") if l == 0 and not main else ("o%d%d" % (l, h),) * 2
+
+    def products(l, hs):
         for t, k in enumerate(("o", "p")):
-            for h in range(H):
-                wait("t", "%s%d%d" % (k, l, h))
+            for h in hs:
+                for sem in own(l, h) if t == 0 else ("p%d%d" % (l, h),):
+                    wait("t", sem)
                 for i in range(2):
                     j = 4 * l + 2 * i + t
                     wait("t", "%s%d" % ("qw" if main else "sw", j // 2))
@@ -136,17 +85,17 @@ def rank_program(g, core, T, topo):
                     if t == 1:
                         ins.then_inc(T.sem["z%d%d%d" % (l, i, h)], 1)
 
-    def tile(l):
+    def tile(l, hs):
         ht = T["h%d" % (l + 1)]
-        for h in range(H):
+        for h in hs:
             a, b, done = 4 * h * cw, 4 * (h + 1) * cw, T.sem["a%d%d" % (l, h)]
             z0, z1 = bank(2 * l * H + h), bank((2 * l + 1) * H + h)
-            wait("v", "z%d0%d" % (l, h))
-            g.vector.tensor_scalar(ht[:, a:b:4], z0, 0.0, C, AluOpType.max, AluOpType.mult).then_inc(done, 1)
-            g.vector.tensor_scalar(ht[:, a + 1:b:4], z0, -C, 0.0, AluOpType.mult, AluOpType.max).then_inc(done, 1)
-            wait("s", "z%d1%d" % (l, h))
-            g.scalar.activation(ht[:, a + 2:b:4], z1, ActivationFunctionType.Relu, scale=C).then_inc(done, 1)
-            g.scalar.activation(ht[:, a + 3:b:4], z1, ActivationFunctionType.Relu, scale=-C).then_inc(done, 1)
+            wait("s", "z%d0%d" % (l, h))
+            g.scalar.activation(ht[:, a:b:4], z0, ActivationFunctionType.Relu, scale=C).then_inc(done, 1)
+            g.scalar.activation(ht[:, a + 1:b:4], z0, ActivationFunctionType.Relu, scale=-C).then_inc(done, 1)
+            wait("v", "z%d1%d" % (l, h))
+            g.vector.tensor_scalar(ht[:, a + 2:b:4], z1, 0.0, C, AluOpType.max, AluOpType.mult).then_inc(done, 1)
+            g.vector.tensor_scalar(ht[:, a + 3:b:4], z1, -C, 0.0, AluOpType.mult, AluOpType.max).then_inc(done, 1)
             wait("v", "a%d%d" % (l, h), 4)
             g.vector.quantize_mx(T["oq%d" % (l + 1)][:, h * cw:h * cw + cw], T["op%d" % (l + 1)][:, h * cw:h * cw + cw],
                                  ht[:, a:b]).then_inc(T.sem["o%d%d" % (l + 1, h)], 1)
@@ -156,87 +105,104 @@ def rank_program(g, core, T, topo):
         g.vector.quantize_mx(T.wq[:, 256 * p:256 * p + 256], T.wp[:, 256 * p:256 * p + 256],
                              T.wt[:, 1024 * p:1024 * p + 1024]).then_inc(T.sem["qw%d" % p], 1)
 
-    names = lambda k: ("wq", "wp") if k == "w" else (k[0] + "q" + k[1], k[0] + "p" + k[1])
-    calls, left = [], {"sent": 0, "gate": 0}
-    for key, waits, outs, first in sorted(plan["steps"][core], key=lambda s: s[0]):
-        mine = "gate" if first and GATE and main else "sent"
-        for part in range(2):
+    def send(outs, mine, parts=(0, 1)):
+        for part in parts:
             trs = []
-            for dst, src_k, dst_k, a, b, there in outs:
-                mask, ne = _engines(topo, core, dst, plan["far"][core], len(outs) == 1)
+            for n, (dst, src_k, dst_k, a, b, there) in enumerate(outs):
+                bits = _bits(topo.mask(core, dst))
+                ne = len(bits) // len(outs)
+                mask = sum(1 << e for e in bits[n * ne:n * ne + ne])
                 rid, pid = topo.addr(dst, core)
-                s_ap, d_ap = T[names(src_k)[part]][:, a:b], T[names(dst_k)[part]][:, a:b]
+                s_ap, d_ap = T[src_k[part]][:, a:b], T[dst_k[part]][:, a:b]
                 if part == 0:
                     s_ap, d_ap = s_ap.bitcast(dt.uint8), d_ap.bitcast(dt.uint8)
-                trs.append((d_ap, s_ap, T.sem[there], pid, rid, mask))
+                trs.append((d_ap, s_ap, T.sem[there[part]], pid, rid, mask))
                 left[mine] += ne
-            calls.append((waits, trs, mine))
-
-    if main:
-        early = plan["early"][r]
-        for h in range(H):
-            g.sync.dma_start(T.xt[:, 4 * h * cw:4 * (h + 1) * cw], T.x[:, 4 * h * cw:4 * (h + 1) * cw]).then_inc(T.sem["lx%d" % h], 16)
-        for p in range(4):
-            if p == 2 and left["gate"]:
-                wait("y", "gate", left["gate"])
-            g.sync.dma_start(T.wt[:, 1024 * p:1024 * p + 1024], T.w[:, 1024 * p:1024 * p + 1024]).then_inc(T.sem["lw%d" % p], 16)
-        g.sync.dma_start(T.vt[:], T.v[:]).then_inc(T.sem.lv, 16)
-        for h in range(H):
-            wait("v", "lx%d" % h, 16)
-            g.vector.quantize_mx(T.oq0[:, h * cw:h * cw + cw], T.op0[:, h * cw:h * cw + cw],
-                                 T.xt[:, 4 * h * cw:4 * (h + 1) * cw]).then_inc(T.sem["o0%d" % h], 1)
-        pack_w(0)
-        pack_w(1)
-        if early:
-            pack_w(2)
-            pack_w(3)
-        products(0)
-        tile(0)
-        if not early:
-            pack_w(2)
-            pack_w(3)
-        products(1)
-        tile(1)
-        wait("v", "lv", 16)
-        g.vector.quantize_mx(T.vq[:], T.vp[:], T.vt[:]).then_inc(T.sem.qv, 1)
-        base = 4 * H if 5 * H <= 8 else 0
-        for t, k in enumerate(("o", "p")):
-            for h in range(H):
-                wait("t", "%s2%d" % (k, h))
-                wait("t", "qv", 1)
-                ins = g.tensor.matmul_mx(bank(base + h), T.vq[:, 128 * t:128 * t + 128], T.vp[:, 128 * t:128 * t + 128],
-                                         T["%sq2" % k][:, h * cw:h * cw + cw], T["%sp2" % k][:, h * cw:h * cw + cw], t == 0, t == 1)
-                if t == 1:
-                    ins.then_inc(T.sem["zy%d" % h], 1)
-        for h in range(H):
-            yv = T.yt[:, h * cw:h * cw + cw]
-            if h % 2 == 0:
-                wait("v", "zy%d" % h, 1)
-                g.vector.tensor_copy(yv, bank(base + h)).then_inc(T.sem["cy%d" % h], 1)
-                wait("y", "cy%d" % h, 1)
-                g.sync.dma_start(T.y[:, h * cw:h * cw + cw], yv).then_inc(T.sem["st%d" % h], 16)
+            if len(trs) == 1:
+                d_ap, s_ap, sem, pid, rid, mask = trs[0]
+                g.remote_dma(d_ap, s_ap, sem, T.sem[mine], pid, rid, mask)
             else:
-                wait("s", "zy%d" % h, 1)
-                g.scalar.activation(yv, bank(base + h), ActivationFunctionType.Copy).then_inc(T.sem["cy%d" % h], 1)
-                wait("s", "cy%d" % h, 1)
-                g.scalar.dma_start(T.y[:, h * cw:h * cw + cw], yv).then_inc(T.sem["st%d" % h], 16)
-        for h in range(H):
-            wait("y" if h % 2 == 0 else "s", "st%d" % h, 16)
-    else:
-        for l in range(2):
-            if maker[l + 1][r] == core:
-                products(l)
-                tile(l)
+                g.remote_dma_fused([RemoteDMATransfer(dst_ids=[DstId(rid=rid, pnc=pid)], dma_engine_mask=mask, remote_sem=sem,
+                                                      src=s_ap, dst=d_ap) for d_ap, s_ap, sem, pid, rid, mask in trs],
+                                   local_sem=T.sem[mine])
 
-    for waits, trs, mine in calls:
-        for sem in waits:
-            wait("g", sem)
-        if len(trs) == 1:
-            d_ap, s_ap, there, pid, rid, mask = trs[0]
-            g.remote_dma(d_ap, s_ap, there, T.sem[mine], pid, rid, mask)
-        else:
-            g.remote_dma_fused([RemoteDMATransfer(dst_ids=[DstId(rid=rid, pnc=pid)], dma_engine_mask=mask, remote_sem=there,
-                                                  src=s_ap, dst=d_ap) for d_ap, s_ap, there, pid, rid, mask in trs],
-                               local_sem=T.sem[mine])
-    if left["sent"]:
+    on = len(_bits(topo.mask(cores[r], lanes[r][0]))) // H
+    for l in range(3):
+        for h in range(H):
+            src = lanes[FROM[l][r]][h]
+            need["p%d%d" % (l, h)] = 2 * len(_bits(topo.mask(src, core)))
+    if not main:
+        need["oc"] = need["os"] = on
+        for p in range(4):
+            need["sw%d" % p] = 2 * on
+
+    O = lambda l: ("oq%d" % l, "op%d" % l)
+    P = lambda l: ("pq%d" % l, "pp%d" % l)
+    W = ("wq", "wp")
+
+    if not main:
+        h = lane
+        for l in range(2):
+            products(l, [h])
+            tile(l, [h])
+        for l in range(3):
+            there = ("p%d%d" % (l, h),) * 2
+            for part in (1, 0) if l == 0 else (0, 1):
+                wait("g", own(l, h)[part])
+                if l < 2:
+                    send([(lanes[to[l]][h], O(l), P(l), h * cw, h * cw + cw, there)], "sent", (part,))
+            send([(cores[to[l]], O(l), P(l), h * cw, h * cw + cw, there)], "sent")
         g.wait_ge(T.sem.sent, left["sent"])
+        return
+
+    hs = list(range(H))
+    for h in hs:
+        wait("g", "o0%d" % h)
+    send([(lanes[r][h], O(0), O(0), h * cw, h * cw + cw, ("oc", "os")) for h in hs], "gate", (1, 0))
+    for p in range(4):
+        wait("g", "qw%d" % p)
+        send([(lanes[r][h], W, W, 256 * p, 256 * p + 256, ("sw%d" % p,) * 2) for h in hs], "gate" if p < 2 else "sent")
+    g.wait_ge(T.sem.sent, left["sent"])
+
+    for h in hs:
+        g.sync.dma_start(T.xt[:, 4 * h * cw:4 * (h + 1) * cw], T.x[:, 4 * h * cw:4 * (h + 1) * cw]).then_inc(T.sem["lx%d" % h], 16)
+    for p in range(4):
+        if p == 2:
+            wait("y", "gate", left["gate"])
+        g.sync.dma_start(T.wt[:, 1024 * p:1024 * p + 1024], T.w[:, 1024 * p:1024 * p + 1024]).then_inc(T.sem["lw%d" % p], 16)
+    g.sync.dma_start(T.vt[:], T.v[:]).then_inc(T.sem.lv, 16)
+
+    for h in hs:
+        wait("v", "lx%d" % h, 16)
+        g.vector.quantize_mx(T.oq0[:, h * cw:h * cw + cw], T.op0[:, h * cw:h * cw + cw],
+                             T.xt[:, 4 * h * cw:4 * (h + 1) * cw]).then_inc(T.sem["o0%d" % h], 1)
+    for p in range(4):
+        pack_w(p)
+    products(0, hs)
+    tile(0, hs)
+    wait("v", "lv", 16)
+    g.vector.quantize_mx(T.vq[:], T.vp[:], T.vt[:]).then_inc(T.sem.qv, 1)
+    products(1, hs)
+    tile(1, hs)
+    for t, k in enumerate(("o", "p")):
+        for h in hs:
+            wait("t", "%s2%d" % (k, h))
+            wait("t", "qv", 1)
+            ins = g.tensor.matmul_mx(bank(h), T.vq[:, 128 * t:128 * t + 128], T.vp[:, 128 * t:128 * t + 128],
+                                     T["%sq2" % k][:, h * cw:h * cw + cw], T["%sp2" % k][:, h * cw:h * cw + cw], t == 0, t == 1)
+            if t == 1:
+                ins.then_inc(T.sem["zy%d" % h], 1)
+    for h in hs:
+        yv = T.yt[:, h * cw:h * cw + cw]
+        if h % 2 == 0:
+            wait("v", "zy%d" % h, 1)
+            g.vector.tensor_copy(yv, bank(h)).then_inc(T.sem["cy%d" % h], 1)
+            wait("y", "cy%d" % h, 1)
+            g.sync.dma_start(T.y[:, h * cw:h * cw + cw], yv).then_inc(T.sem["st%d" % h], 16)
+        else:
+            wait("s", "zy%d" % h, 1)
+            g.scalar.activation(yv, bank(h), ActivationFunctionType.Copy).then_inc(T.sem["cy%d" % h], 1)
+            wait("s", "cy%d" % h, 1)
+            g.scalar.dma_start(T.y[:, h * cw:h * cw + cw], yv).then_inc(T.sem["st%d" % h], 16)
+    for h in hs:
+        wait("y" if h % 2 == 0 else "s", "st%d" % h, 16)

from concourse.bass import DstId, RemoteDMATransfer
from concourse.mybir import dt, AluOpType, ActivationFunctionType

WORLD = 256
NC = 256
H = 2
C = 0.0329

SCRATCH = {
    "xt": ("sbuf", [128, 4 * NC], "bfloat16"),
    "wt": ("sbuf", [128, 4096], "bfloat16"),
    "vt": ("sbuf", [128, 1024], "bfloat16"),
    "wq": ("sbuf", [128, 1024], "float8_e4m3fn_x4"),
    "wp": ("sbuf", [128, 1024], "uint8"),
    "vq": ("sbuf", [128, 256], "float8_e4m3fn_x4"),
    "vp": ("sbuf", [128, 256], "uint8"),
    "h1": ("sbuf", [128, 4 * NC], "bfloat16"),
    "h2": ("sbuf", [128, 4 * NC], "bfloat16"),
    "yt": ("sbuf", [128, NC], "float32"),
    "z": ("psum", [128, 4096], "float32"),
}
for _l in range(3):
    for _k in ("o", "p"):
        SCRATCH["%sq%d" % (_k, _l)] = ("sbuf", [128, NC], "float8_e4m3fn_x4")
        SCRATCH["%sp%d" % (_k, _l)] = ("sbuf", [128, NC], "uint8")

SEMAPHORES = ["sent", "gate", "lv", "qv", "oc", "os"]
SEMAPHORES += ["%s%d" % (k, p) for k in ("lw", "qw", "sw") for p in range(4)]
SEMAPHORES += ["%s%d" % (k, h) for k in ("lx", "zy", "cy", "st") for h in range(2)]
SEMAPHORES += ["%s%d%d" % (k, l, h) for k in ("o", "p") for l in range(3) for h in range(2)]
SEMAPHORES += ["a%d%d" % (l, h) for l in range(2) for h in range(2)]
SEMAPHORES += ["z%d%d%d" % (l, i, h) for l in range(2) for i in range(2) for h in range(2)]


def _lanes(cores, topo, c):
    can = [k for k in range(WORLD) if k not in cores and topo.host(k) == topo.host(c) and topo.chip(k) == topo.chip(c)
           and all(topo.may_write(k, d) for d in cores)]
    near = [k for k in can if topo.die(k) == topo.die(c)]
    away = [k for k in can if topo.die(k) != topo.die(c)]
    return (near + away)[0], (away + near[1:])[0]


def _bits(m):
    return [b for b in range(m.bit_length()) if m >> b & 1]


def rank_program(g, core, T, topo):
    cores, FROM = list(T.cores), T.tables["FROM"]
    here = [r for r, c in enumerate(cores) if topo.host(c) == topo.host(core) and topo.chip(c) == topo.chip(core)]
    if not here:
        return
    r = here[0]
    lanes = [_lanes(cores, topo, c) for c in cores]
    main = core == cores[r]
    if not main and core not in lanes[r]:
        return
    cw = NC // H
    lane = None if main else lanes[r].index(core)
    to = [FROM[l].index(r) for l in range(3)]
    need, seen, left = {}, {}, {"sent": 0, "gate": 0}

    def wait(q, sem, val=None):
        val = need.get(sem, 1) if val is None else val
        if seen.get((q, sem), 0) < val:
            seen[(q, sem)] = val
            {"g": g, "t": g.tensor, "v": g.vector, "s": g.scalar, "y": g.sync}[q].wait_ge(T.sem[sem], val)

    def bank(b):
        return T.z[:, 512 * b:512 * b + cw]

    def own(l, h):
        return ("oc", "os") if l == 0 and not main else ("o%d%d" % (l, h),) * 2

    def products(l, hs):
        for t, k in enumerate(("o", "p")):
            for h in hs:
                for sem in own(l, h) if t == 0 else ("p%d%d" % (l, h),):
                    wait("t", sem)
                for i in range(2):
                    j = 4 * l + 2 * i + t
                    wait("t", "%s%d" % ("qw" if main else "sw", j // 2))
                    ins = g.tensor.matmul_mx(bank((2 * l + i) * H + h), T.wq[:, 128 * j:128 * j + 128], T.wp[:, 128 * j:128 * j + 128],
                                             T["%sq%d" % (k, l)][:, h * cw:h * cw + cw], T["%sp%d" % (k, l)][:, h * cw:h * cw + cw],
                                             t == 0, t == 1)
                    if t == 1:
                        ins.then_inc(T.sem["z%d%d%d" % (l, i, h)], 1)

    def tile(l, hs):
        ht = T["h%d" % (l + 1)]
        for h in hs:
            a, b, done = 4 * h * cw, 4 * (h + 1) * cw, T.sem["a%d%d" % (l, h)]
            z0, z1 = bank(2 * l * H + h), bank((2 * l + 1) * H + h)
            wait("s", "z%d0%d" % (l, h))
            g.scalar.activation(ht[:, a:b:4], z0, ActivationFunctionType.Relu, scale=C).then_inc(done, 1)
            g.scalar.activation(ht[:, a + 1:b:4], z0, ActivationFunctionType.Relu, scale=-C).then_inc(done, 1)
            wait("v", "z%d1%d" % (l, h))
            g.vector.tensor_scalar(ht[:, a + 2:b:4], z1, 0.0, C, AluOpType.max, AluOpType.mult).then_inc(done, 1)
            g.vector.tensor_scalar(ht[:, a + 3:b:4], z1, -C, 0.0, AluOpType.mult, AluOpType.max).then_inc(done, 1)
            wait("v", "a%d%d" % (l, h), 4)
            g.vector.quantize_mx(T["oq%d" % (l + 1)][:, h * cw:h * cw + cw], T["op%d" % (l + 1)][:, h * cw:h * cw + cw],
                                 ht[:, a:b]).then_inc(T.sem["o%d%d" % (l + 1, h)], 1)

    def pack_w(p):
        wait("v", "lw%d" % p, 16)
        g.vector.quantize_mx(T.wq[:, 256 * p:256 * p + 256], T.wp[:, 256 * p:256 * p + 256],
                             T.wt[:, 1024 * p:1024 * p + 1024]).then_inc(T.sem["qw%d" % p], 1)

    def send(outs, mine, parts=(0, 1)):
        for part in parts:
            trs = []
            for n, (dst, src_k, dst_k, a, b, there) in enumerate(outs):
                bits = _bits(topo.mask(core, dst))
                ne = len(bits) // len(outs)
                mask = sum(1 << e for e in bits[n * ne:n * ne + ne])
                rid, pid = topo.addr(dst, core)
                s_ap, d_ap = T[src_k[part]][:, a:b], T[dst_k[part]][:, a:b]
                if part == 0:
                    s_ap, d_ap = s_ap.bitcast(dt.uint8), d_ap.bitcast(dt.uint8)
                trs.append((d_ap, s_ap, T.sem[there[part]], pid, rid, mask))
                left[mine] += ne
            if len(trs) == 1:
                d_ap, s_ap, sem, pid, rid, mask = trs[0]
                g.remote_dma(d_ap, s_ap, sem, T.sem[mine], pid, rid, mask)
            else:
                g.remote_dma_fused([RemoteDMATransfer(dst_ids=[DstId(rid=rid, pnc=pid)], dma_engine_mask=mask, remote_sem=sem,
                                                      src=s_ap, dst=d_ap) for d_ap, s_ap, sem, pid, rid, mask in trs],
                                   local_sem=T.sem[mine])

    on = len(_bits(topo.mask(cores[r], lanes[r][0]))) // H
    for l in range(3):
        for h in range(H):
            src = lanes[FROM[l][r]][h]
            need["p%d%d" % (l, h)] = 2 * len(_bits(topo.mask(src, core)))
    if not main:
        need["oc"] = need["os"] = on
        for p in range(4):
            need["sw%d" % p] = 2 * on

    O = lambda l: ("oq%d" % l, "op%d" % l)
    P = lambda l: ("pq%d" % l, "pp%d" % l)
    W = ("wq", "wp")

    if not main:
        h = lane
        for l in range(2):
            products(l, [h])
            tile(l, [h])
        for l in range(3):
            there = ("p%d%d" % (l, h),) * 2
            for part in (1, 0) if l == 0 else (0, 1):
                wait("g", own(l, h)[part])
                if l < 2:
                    send([(lanes[to[l]][h], O(l), P(l), h * cw, h * cw + cw, there)], "sent", (part,))
            send([(cores[to[l]], O(l), P(l), h * cw, h * cw + cw, there)], "sent")
        g.wait_ge(T.sem.sent, left["sent"])
        return

    hs = list(range(H))
    for h in hs:
        wait("g", "o0%d" % h)
    send([(lanes[r][h], O(0), O(0), h * cw, h * cw + cw, ("oc", "os")) for h in hs], "gate", (1, 0))
    for p in range(4):
        wait("g", "qw%d" % p)
        send([(lanes[r][h], W, W, 256 * p, 256 * p + 256, ("sw%d" % p,) * 2) for h in hs], "gate" if p < 2 else "sent")
    g.wait_ge(T.sem.sent, left["sent"])

    for h in hs:
        g.sync.dma_start(T.xt[:, 4 * h * cw:4 * (h + 1) * cw], T.x[:, 4 * h * cw:4 * (h + 1) * cw]).then_inc(T.sem["lx%d" % h], 16)
    for p in range(4):
        if p == 2:
            wait("y", "gate", left["gate"])
        g.sync.dma_start(T.wt[:, 1024 * p:1024 * p + 1024], T.w[:, 1024 * p:1024 * p + 1024]).then_inc(T.sem["lw%d" % p], 16)
    g.sync.dma_start(T.vt[:], T.v[:]).then_inc(T.sem.lv, 16)

    for h in hs:
        wait("v", "lx%d" % h, 16)
        g.vector.quantize_mx(T.oq0[:, h * cw:h * cw + cw], T.op0[:, h * cw:h * cw + cw],
                             T.xt[:, 4 * h * cw:4 * (h + 1) * cw]).then_inc(T.sem["o0%d" % h], 1)
    for p in range(4):
        pack_w(p)
    products(0, hs)
    tile(0, hs)
    wait("v", "lv", 16)
    g.vector.quantize_mx(T.vq[:], T.vp[:], T.vt[:]).then_inc(T.sem.qv, 1)
    products(1, hs)
    tile(1, hs)
    for t, k in enumerate(("o", "p")):
        for h in hs:
            wait("t", "%s2%d" % (k, h))
            wait("t", "qv", 1)
            ins = g.tensor.matmul_mx(bank(h), T.vq[:, 128 * t:128 * t + 128], T.vp[:, 128 * t:128 * t + 128],
                                     T["%sq2" % k][:, h * cw:h * cw + cw], T["%sp2" % k][:, h * cw:h * cw + cw], t == 0, t == 1)
            if t == 1:
                ins.then_inc(T.sem["zy%d" % h], 1)
    for h in hs:
        yv = T.yt[:, h * cw:h * cw + cw]
        if h % 2 == 0:
            wait("v", "zy%d" % h, 1)
            g.vector.tensor_copy(yv, bank(h)).then_inc(T.sem["cy%d" % h], 1)
            wait("y", "cy%d" % h, 1)
            g.sync.dma_start(T.y[:, h * cw:h * cw + cw], yv).then_inc(T.sem["st%d" % h], 16)
        else:
            wait("s", "zy%d" % h, 1)
            g.scalar.activation(yv, bank(h), ActivationFunctionType.Copy).then_inc(T.sem["cy%d" % h], 1)
            wait("s", "cy%d" % h, 1)
            g.scalar.dma_start(T.y[:, h * cw:h * cw + cw], yv).then_inc(T.sem["st%d" % h], 16)
    for h in hs:
        wait("y" if h % 2 == 0 else "s", "st%d" % h, 16)
